import numpy as np
CORES = [8,80,112,136,208,240,264,336,368,392,464,496]
N = 12
V, DEP = 16384, 16
def entries(a): return a.T.reshape(-1)
def pack(v, P): return np.ascontiguousarray(np.asarray(v, np.int32).reshape(-1, P).T)
def forest(rng, n, lev):
    P = np.arange(n)
    for l in range(1, int(lev.max()) + 1):
        a, b = np.nonzero(lev == l)[0], np.nonzero(lev == l - 1)[0]; P[a] = b[rng.integers(0, len(b), len(a))]
    return P
def lists(rng, how):
    n = N * V; P = np.arange(n)
    if how == "uniform":
        lev = rng.integers(0, DEP + 1, n); lev[rng.permutation(n)[:DEP + 1]] = np.arange(DEP + 1); P = forest(rng, n, lev)
    if how == "star":
        lev = np.ones(n, np.int64); lev[rng.permutation(n)[:4]] = 0; P = forest(rng, n, lev)
    if how == "chain":
        W = np.stack([V * r + rng.permutation(V)[:V // (DEP + 1) * (DEP + 1)].reshape(-1, DEP + 1) for r in range(N)]); P[W[:, :, 1:]] = np.roll(W, 1, axis=0)[:, :, :-1]
    if how == "deep":
        z = rng.permutation(N); g = V * z[1 + np.arange(DEP) % (N - 1)] + rng.permutation(V)[:DEP]; P[:] = g[-1]; P[g] = np.concatenate([g[:1], g[:-1]])
    if how == "whole":
        o = rng.permutation(N)
        for i in range(1, N - 1):
            if i % (DEP + 1): P[V * o[i]:V * o[i] + V] = V * o[i - 1] + rng.permutation(V)
        P[V * o[-1]:V * o[-1] + V] = V * o[-1] + forest(rng, V, rng.permutation(np.concatenate([np.arange(DEP + 1), rng.integers(0, DEP + 1, V - DEP - 1)])))
    return {"par": np.stack([pack(p, 16) for p in P.reshape(N, V)])}
def setup_inputs(rng):
    return dict({"val": rng.standard_normal((N, 16, V // 16), dtype=np.float32)}, **lists(rng, "uniform"))
def setup_inputs_chain(rng):
    d = setup_inputs(rng); d.update(lists(rng, "chain"))
    for k in ("val",): d[k] = (d[k].astype(np.float32) * 1048576.0).astype(d[k].dtype)
    return d
def setup_inputs_deep(rng):
    d = setup_inputs(rng); d.update(lists(rng, "deep"))
    for k in ("val",): d[k] = (d[k].astype(np.float32) * (1 / 1024.0)).astype(d[k].dtype)
    return d
def setup_inputs_star(rng):
    d = setup_inputs(rng); d.update(lists(rng, "star"))
    return d
def setup_inputs_whole(rng):
    d = setup_inputs(rng); d.update(lists(rng, "whole"))
    return d
def check_inputs(x):
    bad = []
    if x["par"].min() < 0 or x["par"].max() >= N * V: bad.append("par out of range")
    p = np.concatenate([entries(a) for a in x["par"]]); q = p
    for k in range(DEP - 1): q = p[q]
    if (p[q] != q).any(): bad.append("a node is more than DEP hops from a root")
    return bad
def reference(val, par):
    p = np.concatenate([entries(a) for a in par]); v = np.concatenate([entries(a) for a in val])
    q = p
    for k in range(DEP - 1): q = p[q]
    return {"y": np.stack([np.ascontiguousarray(v[q][V * r:V * r + V].reshape(-1, 16).T) for r in range(N)])}

from concourse.bass import DstId, RemoteDMATransfer
from concourse.mybir import AluOpType, AxisListType, ActivationFunctionType

SCRATCH = {
    "lndv": ("dram", [12, 128, 32], "float32"),
    "tab": ("dram", [8, 128, 384], "bfloat16"),
    "tab2": ("dram", [8, 128, 384], "bfloat16"),
    "tabv": ("dram", [4, 128, 384], "float32"),
    "osh": ("dram", [128, 64], "bfloat16"),
    "p4": ("dram", [4, 128, 16], "bfloat16"),
    "vst": ("dram", [4, 128, 32], "float32"),
    "ybuf": ("dram", [8, 128, 16], "float32"),
    "praw": ("sbuf", [128, 256], "int32"),
    "pin": ("sbuf", [128, 64], "int32"),
    "enc": ("sbuf", [128, 1152], "int32"),
    "fw": ("sbuf", [128, 768], "bfloat16"),
    "fw2": ("sbuf", [128, 768], "bfloat16"),
    "fwv": ("sbuf", [128, 384], "float32"),
    "win": ("sbuf", [128, 12288], "bfloat16"),
    "win2": ("sbuf", [128, 12288], "bfloat16"),
    "vwin": ("sbuf", [128, 12288], "float32"),
    "mi": ("sbuf", [128, 128], "int32"),
    "mdiv": ("sbuf", [128, 128], "int32"),
    "mmod": ("sbuf", [128, 128], "int32"),
    "pi": ("sbuf", [128, 4], "int32"),
    "pcols": ("sbuf", [128, 16], "int32"),
    "fcols": ("sbuf", [128, 24], "float32"),
    "bd": ("sbuf", [128, 128], "float32"),
    "cc": ("sbuf", [128, 128], "float32"),
    "cd": ("sbuf", [128, 128], "float32"),
    "idb": ("sbuf", [128, 128], "bfloat16"),
    "idf": ("sbuf", [128, 128], "float32"),
    "wsel": ("sbuf", [128, 2048], "bfloat16"),
    "wb": ("sbuf", [128, 128], "bfloat16"),
    "wx": ("sbuf", [128, 8], "bfloat16"),
    "cm": ("sbuf", [128, 128], "bfloat16"),
    "ones": ("sbuf", [128, 512], "bfloat16"),
    "qab": ("sbuf", [128, 32], "bfloat16"),
    "qx": ("sbuf", [128, 512], "bfloat16"),
    "xx": ("sbuf", [128, 512], "bfloat16"),
    "ex": ("sbuf", [128, 32], "bfloat16"),
    "mk": ("sbuf", [128, 512], "bfloat16"),
    "off": ("sbuf", [128, 32], "uint16"),
    "s1": ("sbuf", [128, 512], "float32"),
    "s2": ("sbuf", [128, 512], "float32"),
    "t1": ("sbuf", [128, 512], "float32"),
    "yt": ("sbuf", [128, 16], "float32"),
    "e0": ("psum", [128, 512], "float32"),
    "zz": ("psum", [128, 512], "float32"),
    "ez": ("psum", [128, 512], "float32"),
    "tp0": ("psum", [128, 512], "float32"),
    "tp1": ("psum", [128, 512], "float32"),
    "tp2": ("psum", [128, 512], "float32"),
    "tp3": ("psum", [128, 512], "float32"),
}
SEMAPHORES = ["pld", "vld", "par_in", "val_in", "encs", "encf", "cab", "near", "far", "own", "tn", "tf", "cpn", "cpf", "osl",
              "exin", "exl", "p4l", "cab2", "near2", "far2", "tn2", "tf2", "cpn2", "cpf2", "wld2",
              "vcab", "vnear", "vfar", "vt", "fvl", "cpv",
              "ls", "io0", "cv", "cw", "vz", "qld", "qc", "wld", "vwl",
              "g0", "m1", "of", "b0", "zc", "xz", "xs", "sa", "sb", "fin", "tp", "yv", "yin", "yst"]

CORES_ALL = 512
BIG = 402653184.0
HALFMAX = (2.0 - 2.0 ** -23) * 2.0 ** 63


def bits(m):
    return [1 << b for b in range(16) if (m >> b) & 1]


def split(m, n, k):
    b = bits(m)
    return [sum(b[i * k:(i + 1) * k]) for i in range(n)]


def chip_cores(c, topo):
    return [c] + [d for d in range(CORES_ALL) if d != c and topo.host(d) == topo.host(c) and topo.chip(d) == topo.chip(c)]


def rank_program(g, core, T, topo):
    ranks = T.cores
    r = None
    for i, c in enumerate(ranks):
        if topo.host(c) == topo.host(core) and topo.chip(c) == topo.chip(core):
            r = i
    if r is None:
        return
    chips = [chip_cores(c, topo) for c in ranks]
    mine = chips[r]
    w = mine.index(core)

    def relays(i):
        mate = [d for d in range(CORES_ALL) if topo.mates(chips[i][0], d)][0]
        return [d for d in chips[i] if topo.may_write(d, mate)]
    rel = [relays(i) for i in range(len(ranks))]
    kk = rel[r].index(core) if core in rel[r] else None
    rack = [topo.rack(topo.host(c)) for c in ranks]
    near = [i for i in range(len(ranks)) if i != r and rack[i] == rack[r]]
    partner = [j for j in range(len(ranks)) if rack[j] != rack[r] and topo.chip(ranks[j]) == topo.chip(ranks[r])
               and topo.may_write(ranks[r], ranks[j])][0]
    my = rack[r]

    def did(d):
        rid, pid = topo.addr(d, core)
        return DstId(rid=rid, pnc=pid)

    def xfer(dsts, m, rs, src, dst):
        return RemoteDMATransfer(dst_ids=[did(d) for d in dsts], dma_engine_mask=m, remote_sem=rs,
                                 srcs=[src], dsts=[dst] * len(dsts))
    peers = [d for d in mine if d != core]
    on = topo.mask(core, peers[0])
    S = T.sem
    A = AluOpType
    V = g.vector
    PE = g.tensor
    from_rel = 3 if kk is not None else 4
    home_rel = rel[r][w // 2]
    home = home_rel == core
    hf = w % 2

    g.iota(T.pi[:, 0:1], [[1, 1]], 0, 1).then_inc(S.io0, 1)
    g.iota(T.mi[:], [[1, 128]], 0, 0).then_inc(S.io0, 1)

    if w == 0:
        for k in range(4):
            for q, p0 in ((g.sync, 0), (g.scalar, 64)):
                q.dma_start(T.praw[p0:p0 + 64, 64 * k:64 * k + 64], T.par[4 * k:4 * k + 4, :]).then_inc(S.pld, 16)
        g.sync.dma_start(T.vst[:], T.val[:]).then_inc(S.vld, 16)
        ms = split(on, 4, 4)
        g.wait_ge(S.pld, 128)
        g.remote_dma_fused([xfer([rel[r][k]], ms[k], S.par_in, T.praw[:, 64 * k:64 * k + 64], T.pin[:]) for k in range(4)], local_sem=S.ls)
        g.wait_ge(S.vld, 16)
        g.remote_dma_fused([xfer([rel[r][k]], ms[k], S.val_in, T.vst[k], T.lndv[r]) for k in range(4)], local_sem=S.ls)

    ncv = [0]

    def cv(ins):
        ins.then_inc(S.cv, 1)
        ncv[0] += 1

    def cvw():
        V.wait_ge(S.cv, ncv[0])
    fc = [T.fcols[:, 4 * i:4 * i + 1] for i in range(6)]
    pc = [T.pcols[:, 4 * i:4 * i + 1] for i in range(4)]
    cv(V.memset(T.cm[0:1, :], -15.5))
    cv(V.memset(T.ones[0:1, :], 1.0))
    cv(V.memset(T.qx[:], 0.0))
    V.wait_ge(S.io0, 2)
    cv(V.tensor_scalar(T.mdiv[:], T.mi[:], 5, None, A.arith_shift_right))
    cv(V.tensor_scalar(T.mmod[:], T.mi[:], 15, None, A.bitwise_and))
    cv(V.tensor_scalar(pc[0], T.pi[:, 0:1], 5, None, A.arith_shift_right))
    cv(V.tensor_scalar(pc[1], T.pi[:, 0:1], 4, 1, A.arith_shift_right, A.bitwise_and))
    cv(V.tensor_scalar(pc[2], T.pi[:, 0:1], 15, None, A.bitwise_and))
    cv(V.tensor_copy(fc[4], T.pi[:, 0:1]))
    cvw()
    cv(V.tensor_copy(fc[0], pc[0]))
    cv(V.tensor_scalar(fc[1], pc[1], 31.0, 1.0, A.mult, A.add))
    cv(V.tensor_scalar(fc[2], pc[1], -1.0, 1.0, A.mult, A.add))
    cv(V.tensor_scalar(fc[3], pc[2], 32.0, BIG - 256.0, A.mult, A.add))
    cv(V.tensor_copy(fc[5], pc[1]))
    cv(V.tensor_scalar(T.cc[:], T.mmod[:], 1.0, None, A.add))
    cvw()
    cv(V.tensor_scalar(T.bd[:], T.mdiv[:], fc[0], None, A.is_equal))
    cvw()
    cv(V.tensor_tensor(T.cd[:], T.cc[:], T.bd[:], A.mult))
    cv(V.tensor_scalar(T.wb[:], T.bd[:], fc[2], None, A.mult))
    cvw()

    nls = 0
    parts = ((my, S.near, S.cpn, S.tn), (1 - my, S.far, S.cpf, S.tf))
    parts2 = ((my, S.near2, S.cpn2, S.tn2), (1 - my, S.far2, S.cpf2, S.tf2))

    def col(f, i):
        return f[:, 64 * i:64 * i + 64]
    if kk is not None:
        ne = [0]
        E = [T.enc[:, 64 * i:64 * i + 64] for i in range(18)]

        def en(ins):
            ins.then_inc(S.encs, 1)
            ne[0] += 1

        def enw():
            V.wait_ge(S.encs, ne[0])
        P = T.pin[:]
        R, w7, v, b0, x6, b9, k8, c1, c2, c3, k20, q, d1, d2, e, a1, d3 = E[:17]
        V.wait_ge(S.par_in, 4)
        en(V.tensor_scalar(R, P, 14, None, A.arith_shift_right))
        en(V.tensor_scalar(b0, P, 1, None, A.bitwise_and))
        en(V.tensor_scalar(x6, P, 10, 15, A.arith_shift_right, A.bitwise_and))
        en(V.tensor_scalar(w7, P, 1, 7, A.arith_shift_right, A.bitwise_and))
        en(V.tensor_scalar(b9, P, 9, 1, A.arith_shift_right, A.bitwise_and))
        en(V.tensor_scalar(v, P, 4, 31, A.arith_shift_right, A.bitwise_and))
        enw()
        en(V.tensor_scalar(k8, R, 6.0, 8.0, A.is_ge, A.mult))
        en(V.tensor_scalar(k20, R, 6.0, 20.0, A.is_ge, A.mult))
        en(V.tensor_scalar(c1, b0, 192.0, -184.0, A.mult, A.add))
        en(V.tensor_scalar(c2, x6, 12.0, None, A.mult))
        en(V.tensor_scalar(c3, R, 2.0, None, A.mult))
        enw()
        en(V.tensor_tensor(q, k8, w7, A.add))
        en(V.tensor_tensor(d1, c1, c2, A.add))
        en(V.tensor_tensor(d2, c3, b9, A.add))
        en(V.tensor_tensor(e, k20, w7, A.add))
        enw()
        en(V.tensor_scalar(a1, q, 32.0, -256.0, A.mult, A.add))
        en(V.tensor_tensor(d3, d1, d2, A.add))
        enw()
        V.tensor_tensor(T.fw[0:64, 64 * r:64 * r + 64], T.enc[0:64, 960:1024], T.enc[0:64, 128:192], A.add).then_inc(S.encf, 1)
        V.tensor_tensor(T.fw[64:128, 64 * r:64 * r + 64], T.enc[64:128, 1024:1088], T.enc[64:128, 896:960], A.subtract).then_inc(S.encf, 1)

        offm = topo.mask(core, rel[partner][kk])
        onm = on & ~offm
        n_off, n_on, n_all = len(bits(offm)), len(bits(onm)), len(bits(on))
        across = [rel[partner][kk]]
        around = [rel[i][kk] for i in near]
        owners = [mine[2 * kk + i] for i in range(2) if mine[2 * kk + i] != core]

        def fused(*xs):
            g.remote_dma_fused(list(xs), local_sem=S.ls)
        L, F = T.lndv, T.fw
        g.wait_ge(S.encf, 2)
        fused(xfer(across, offm, S.cab, col(F, r), col(F, r)))
        fused(xfer(around, offm, S.near, col(F, r), col(F, r)), xfer(owners, onm, S.own, col(F, r), T.osh[:]))
        g.wait_ge(S.val_in, 4)
        fused(xfer(across, offm, S.vcab, L[r], L[r]))
        g.wait_ge(S.cab, n_off)
        fused(xfer(around, offm, S.far, col(F, partner), col(F, partner)))
        fused(xfer(around, offm, S.vnear, L[r], L[r]))
        g.wait_ge(S.near, 5 * n_off)
        fused(xfer(peers, on, S.tn, F[:, 384 * my:384 * my + 384], T.tab[4 * my + kk]))
        g.wait_ge(S.vcab, n_off)
        fused(xfer(around, offm, S.vfar, L[partner], L[partner]))
        g.wait_ge(S.far, 5 * n_off)
        fused(xfer(peers, on, S.tf, F[:, 384 * (1 - my):384 * (1 - my) + 384], T.tab[4 * (1 - my) + kk]))
        g.wait_ge(S.fvl, 12 * 16)
        fused(xfer(peers, on, S.vt, T.fwv[:], T.tabv[kk]))
        nls = 6 * n_off + n_on + 3 * n_all

    for s in range(16):
        V.tensor_scalar(T.wsel[:, 128 * s:128 * s + 128], T.cd[:], float(s + 1), fc[1], A.is_equal, A.mult).then_inc(S.cw, 1)
    V.tensor_scalar(T.idb[:], T.mi[:], fc[4], None, A.is_equal).then_inc(S.cw, 1)
    V.tensor_scalar(T.idf[:], T.mi[:], fc[4], None, A.is_equal).then_inc(S.cw, 1)
    V.tensor_scalar(T.wx[:, 0:4], T.mi[:, 0:4], fc[0], fc[2], A.is_equal, A.mult).then_inc(S.cw, 1)
    V.tensor_scalar(T.wx[:, 4:8], T.mi[:, 0:4], fc[0], fc[5], A.is_equal, A.mult).then_inc(S.cw, 1)
    for c in range(2):
        V.memset(T.vwin[:, 3072 * c:3072 * c + 3072], 0.0).then_inc(S.vz, 1)
    g.scalar.wait_ge(S.cw, 20)
    for c in range(3, 6):
        g.scalar.activation(T.vwin[:, 2048 * c:2048 * c + 2048], T.wsel[:], ActivationFunctionType.Copy, scale=0.0).then_inc(S.vz, 1)

    if home:
        g.sync.wait_ge(S.encf, 2)
        g.sync.dma_start(T.osh[:], col(T.fw, r)).then_inc(S.osl, 16)
    for q, pp in ((g.sync, 0), (g.scalar, 1)):
        if home:
            q.wait_ge(S.osl, 16)
        else:
            q.wait_ge(S.own, 8)
        p0 = 64 * pp + 32 * hf
        q.dma_start(T.qab[:, 16 * pp:16 * pp + 16], T.osh[p0:p0 + 32, :]).then_inc(S.qld, 16)

    def expand(pts, fw, tab, win, ready, cab, wld):
        for n, (rk, arr, cps, ts) in enumerate(pts):
            if kk is not None:
                g.scalar.wait_ge(arr, 40)
                if n == 0:
                    g.scalar.wait_ge(*ready)
                else:
                    g.scalar.wait_ge(cab, 8)
                g.scalar.dma_start(tab[4 * rk + kk], fw[:, 384 * rk:384 * rk + 384]).then_inc(cps, 16)
            for q, pp in ((g.sync, 0), (g.scalar, 1)):
                q.wait_ge(ts, 16 * from_rel)
                if kk is not None:
                    q.wait_ge(cps, 16)
                for c in range(4):
                    p0 = 32 * c + 16 * pp + 8 * rk
                    q.dma_start(win[p0:p0 + 8, :], tab[4 * rk:4 * rk + 4, 64 * pp:64 * pp + 64, :]).then_inc(wld, 16)
    expand(parts, T.fw, T.tab, T.win, (S.encf, 2), S.cab, S.wld)
    if kk is not None:
        g.sync.wait_ge(S.val_in, 4)
        g.sync.wait_ge(S.vnear, 40)
        g.sync.wait_ge(S.vcab, 8)
        g.sync.wait_ge(S.vfar, 40)
        for i in range(len(ranks)):
            rk, c = i // 6, i % 6
            g.sync.dma_start(T.fwv[64 * rk:64 * rk + 64, 64 * c:64 * c + 64], T.lndv[i]).then_inc(S.fvl, 16)
        g.sync.wait_ge(S.fvl, 12 * 16)
        g.sync.dma_start(T.tabv[kk], T.fwv[:]).then_inc(S.cpv, 16)

    if home:
        for q, pp in ((g.sync, 0), (g.scalar, 1)):
            q.wait_ge(S.xs, 1)
            q.dma_start(T.p4[2 * pp + hf], T.ex[:, 16 * pp:16 * pp + 16]).then_inc(S.exl, 16)
    else:
        ms = split(on, 2, 4)
        g.wait_ge(S.xs, 1)
        g.remote_dma_fused([xfer([home_rel], ms[pp], S.exin, T.ex[:, 16 * pp:16 * pp + 16], T.p4[2 * pp + hf]) for pp in range(2)],
                           local_sem=S.ls)
        nls += 8
    if kk is not None:
        g.sync.wait_ge(S.exin, 8 * len(owners))
        if len(owners) == 1:
            g.sync.wait_ge(S.exl, 32)
        g.sync.dma_start(col(T.fw2, r), T.p4[:]).then_inc(S.p4l, 16)
        F = T.fw2
        g.wait_ge(S.p4l, 16)
        fused(xfer(across, offm, S.cab2, col(F, r), col(F, r)))
        fused(xfer(around, offm, S.near2, col(F, r), col(F, r)))
        g.wait_ge(S.cab2, n_off)
        fused(xfer(around, offm, S.far2, col(F, partner), col(F, partner)))
        for rk, arr, _, ts in parts2:
            g.wait_ge(arr, 5 * n_off)
            fused(xfer(peers, on, ts, F[:, 384 * rk:384 * rk + 384], T.tab2[4 * rk + kk]))
        nls += 3 * n_off + 2 * n_all
    g.sync.wait_ge(S.vz, 5)
    g.sync.wait_ge(S.vt, 16 * from_rel)
    if kk is not None:
        g.sync.wait_ge(S.cpv, 16)
    for rk in range(2):
        for c in range(4):
            p0 = 32 * c + 8 * rk
            g.sync.dma_start(T.vwin[p0:p0 + 8, :], T.tabv[:, 64 * rk:64 * rk + 64, :]).then_inc(S.vwl, 16)
    expand(parts2, T.fw2, T.tab2, T.win2, (S.p4l, 16), S.cab2, S.wld2)

    TP = [T.tp0, T.tp1, T.tp2, T.tp3]
    V.wait_ge(S.qld, 32)
    V.tensor_copy(T.qx[:, 0:512:32], T.qab[:, 0:16]).then_inc(S.qc, 1)
    V.tensor_copy(T.qx[:, 16:512:32], T.qab[:, 16:32]).then_inc(S.qc, 1)
    PE.wait_ge(S.cv, ncv[0])
    PE.wait_ge(S.cw, 20)
    PE.wait_ge(S.qc, 2)
    for c in range(4):
        PE.matmul(T.tp0[:, 128 * c:128 * c + 128], T.qx[:, 128 * c:128 * c + 128], T.idb[:], True, True).then_inc(S.tp, 1)
    V.wait_ge(S.tp, 4)

    HOPS = 7
    for step in range(HOPS):
        if step == 0:
            V.tensor_copy(T.xx[:], T.tp0[:]).then_inc(S.g0, 1)
        else:
            if step == 1:
                V.wait_ge(S.wld, 16 * 16)
            if step == 4:
                V.wait_ge(S.wld2, 16 * 16)
            V.wait_ge(S.m1, step)
            V.wait_ge(S.of, step)
            win = T.win if step < 4 else T.win2
            V.tensor_tensor(T.xx[:], win[:, 0:12288].indirect(T.off[:]), T.mk[:], A.mult).then_inc(S.g0, 1)
            PE.wait_ge(S.m1, step)
        PE.matmul(T.e0[:], T.cm[0:1, :], T.ones[0:1, :], True, False)
        PE.wait_ge(S.g0, step + 1)
        if step == 3:
            for c in range(4):
                for pp in range(2):
                    z = 16 * pp + 4 * c
                    ins = PE.matmul(T.ez[:, z:z + 4], T.xx[:, 128 * c:128 * c + 128], T.wx[:, 4 * pp:4 * pp + 4], True, True)
                    ins.then_inc(S.xz, 1)
        PE.matmul(T.e0[:], T.wb[:], T.xx[:], False, True).then_inc(S.b0, 1)
        for s in range(16):
            ins = PE.matmul(T.zz[:, 0:32], T.wsel[:, 128 * s:128 * s + 128], T.xx[:, s:512:16], s == 0, s == 15)
        ins.then_inc(S.zc, 1)
        if step == 3:
            V.wait_ge(S.xz, 8)
            V.tensor_copy(T.ex[:], T.ez[:, 0:32]).then_inc(S.xs, 1)
        V.wait_ge(S.b0, step + 1)
        V.tensor_scalar(T.mk[:], T.e0[:], BIG, fc[3], A.add, A.is_equal).then_inc(S.m1, 1)
        V.wait_ge(S.zc, step + 1)
        V.tensor_scalar(T.off[:], T.zz[:, 0:32], 6144.0, None, A.add).then_inc(S.of, 1)

    g.scalar.wait_ge(S.m1, HOPS)
    g.scalar.activation(T.s1[:], T.mk[:], ActivationFunctionType.Identity, bias=-HALFMAX, scale=2 * HALFMAX).then_inc(S.sa, 1)
    g.scalar.wait_ge(S.sa, 1)
    g.scalar.activation(T.s2[:], T.s1[:], ActivationFunctionType.Copy, scale=2.0 ** 64).then_inc(S.sb, 1)
    V.wait_ge(S.sb, 1)
    V.wait_ge(S.of, HOPS)
    V.wait_ge(S.vwl, 8 * 16)
    V.tensor_tensor(T.t1[:], T.vwin[:, 0:12288].indirect(T.off[:]), T.s2[:], A.min).then_inc(S.fin, 1)
    PE.wait_ge(S.fin, 1)
    for c in range(4):
        PE.transpose(TP[c][:, 0:128], T.t1[:, 128 * c:128 * c + 128], T.idf[:]).then_inc(S.tp, 1)
    for c in range(4):
        V.wait_ge(S.tp, 5 + c)
        for i in range(4):
            b = 4 * c + i
            V.tensor_reduce(T.yt[:, b:b + 1], TP[c][:, 32 * i:32 * i + 16], AxisListType.X, A.max).then_inc(S.yv, 1)
    if w == 0:
        g.sync.wait_ge(S.yv, 16)
        g.sync.dma_start(T.y[0:2, :], T.yt[:]).then_inc(S.yst, 16)
        g.sync.wait_ge(S.yin, 7 * 8)
        g.sync.dma_start(T.y[2:16, :], T.ybuf[1:8]).then_inc(S.yst, 16)
        g.sync.wait_ge(S.yst, 32)
        g.wait_ge(S.ls, 32 + nls)
    else:
        g.wait_ge(S.yv, 16)
        g.remote_dma_fused([xfer([mine[0]], split(on, 1, 8)[0], S.yin, T.yt[:], T.ybuf[w])], local_sem=S.ls)
        g.wait_ge(S.ls, 8 + nls)
